import numpy as np
import ml_dtypes


def mxq(x, axis, fmt="e4m3"):
    dtype, down = {"e4m3": (ml_dtypes.float8_e4m3fn, 7), "e5m2": (ml_dtypes.float8_e5m2, 14)}[fmt]
    v = np.moveaxis(np.asarray(x, np.float32).astype(ml_dtypes.bfloat16).astype(np.float64), axis, -1)
    blocks = v.reshape(v.shape[:-1] + (-1, 32))
    amax = np.abs(blocks).max(-1, keepdims=True)
    byte = np.maximum(np.where(amax > 0, np.frexp(amax)[1] - 1 + 127, 0) - down, 1)
    scale = np.exp2(byte - 127.0)
    codes = (blocks / scale).astype(np.float32).astype(dtype).astype(np.float64)
    return np.moveaxis((codes * scale).reshape(v.shape), -1, axis)


WIDE = False


def mx_kscale(k):
    if not WIDE:
        return np.ones(k)
    levels = np.array([10, -10, 5, -5, 0])
    if k % 512:
        return np.exp2(np.random.permutation(np.resize(levels, k // 32))).repeat(32)
    a = np.empty((k // 512, 16))
    for p in range(k // 512):
        a[p, :8] = np.random.permutation(np.resize(levels, 8))
        for g in range(8):
            far = levels[np.abs(levels - a[p, g]) >= 10]
            a[p, g + 8] = far[np.random.randint(len(far))]
    return np.exp2(a.ravel()).repeat(32)


def f64(x):
    return np.asarray(x).astype(np.float64)


def striped(idx):
    return np.tile(idx.reshape(-1, 16).T, (8, 1)).astype(np.uint16)


def unstriped(offs):
    return offs[:16].T.reshape(-1).astype(np.int64)


E2M1 = np.array([0.0, 0.5, 1.0, 1.5, 2.0, 3.0, 4.0, 6.0, -0.0, -0.5, -1.0, -1.5, -2.0, -3.0, -4.0, -6.0])


def pack_weight(w, fmt):
    k, n = w.shape
    w = f64(np.asarray(w, np.float32).astype(ml_dtypes.bfloat16)).reshape(k // 32, 32, n)
    amax = np.abs(w).max(1)
    if fmt == "e4m3":
        byte = np.frexp(amax)[1] - 1 + 127 - 7
    else:
        mant, ex = np.frexp(amax / 6.0)
        byte = np.where(mant > 0.5, ex, ex - 1) + 127
    byte = np.clip(np.where(amax > 0, byte, 1), 1, 254)
    scaled = (w * np.exp2(127.0 - byte)[:, None, :]).reshape(k, n).astype(np.float32)
    by_word = np.ascontiguousarray(scaled.reshape(k // 512, 128, 4, n).transpose(0, 1, 3, 2))
    if fmt == "e4m3":
        words = by_word.astype(ml_dtypes.float8_e4m3fn).view(np.uint8)
    else:
        c = by_word.astype(ml_dtypes.float4_e2m1fn).view(np.uint8) & 0xF
        words = (c[..., 0::2] | (c[..., 1::2] << 4)).reshape(k // 512, 128, 2 * n)
    return np.ascontiguousarray(words), np.ascontiguousarray(byte.astype(np.uint8).reshape(k // 512, 16, n))


def unpack_weight(words, scales, fmt):
    g, _, n = scales.shape
    words = np.ascontiguousarray(words).reshape(g, 128, n, -1)
    if fmt == "e4m3":
        vals = words.view(ml_dtypes.float8_e4m3fn).astype(np.float64)
    else:
        nib = np.empty((g, 128, n, 4), np.uint8)
        nib[..., 0::2] = words & 0xF
        nib[..., 1::2] = words >> 4
        vals = E2M1[nib]
    vals = vals * np.repeat(np.exp2(scales.astype(np.float64) - 127.0), 8, axis=1)[..., None]
    return vals.transpose(0, 1, 3, 2).reshape(g * 512, n)


def gelu(v):
    return 0.5 * v * (1.0 + np.tanh(np.sqrt(2.0 / np.pi) * (v + 0.044715 * v**3)))


K, T, E, C, H, N = 512, 1024, 4, 128, 1024, 512
R = 4


def by_expert(wq, xq):
    return np.concatenate([wq[e].T @ xq[:, e * C:(e + 1) * C] for e in range(E)], axis=1)


def setup_inputs():
    n = np.random.standard_normal
    s = mx_kscale(K)[:, None]
    u = mx_kscale(H)
    slot_token = np.concatenate([r * (T // R) + np.random.permutation(T // R)[:C // R] for e in range(E) for r in range(R)])
    w1 = [pack_weight(m, "e2m1") for m in n((E, K, H)) / np.sqrt(K) / s[None]]
    w3 = [pack_weight(m, "e2m1") for m in n((E, K, H)) / np.sqrt(K) / s[None] * u[None, None, :]]
    w2 = [pack_weight(m, "e2m1") for m in n((E, H, N)) / np.sqrt(H) / u[None, :, None]]
    x = pack_weight(n((K, T)) * s, "e4m3")
    return {
        "x_words": x[0],
        "x_scales": x[1],
        "w1_words": np.stack([m[0] for m in w1]),
        "w1_scales": np.stack([m[1] for m in w1]),
        "w3_words": np.stack([m[0] for m in w3]),
        "w3_scales": np.stack([m[1] for m in w3]),
        "w2_words": np.stack([m[0] for m in w2]),
        "w2_scales": np.stack([m[1] for m in w2]),
        "offs": striped(slot_token),
    }


def reference(x_words, x_scales, w1_words, w1_scales, w3_words, w3_scales, w2_words, w2_scales, offs):
    idx = unstriped(offs)
    w1 = np.stack([unpack_weight(w1_words[e], w1_scales[e], "e2m1") for e in range(E)])
    w3 = np.stack([unpack_weight(w3_words[e], w3_scales[e], "e2m1") for e in range(E)])
    w2 = np.stack([unpack_weight(w2_words[e], w2_scales[e], "e2m1") for e in range(E)])
    xq = unpack_weight(x_words, x_scales, "e4m3")[:, idx]
    h = gelu(by_expert(w1, xq))
    h = h * by_expert(w3, xq)
    y = by_expert(w2, mxq(h, 0, "e4m3"))
    return y.reshape(N, E, R, C // R).transpose(0, 2, 1, 3).reshape(N, E * C)

@@ -1,0 +1,218 @@
+from contextlib import ExitStack
+
+import concourse.mybir as mybir
+from concourse.masks import make_identity
+
+K, T, E, C, H, N = 512, 1024, 4, 128, 1024, 512
+R = 4
+FLOPS = 2 * E * C * (2 * K * H + H * N)
+
+F32 = mybir.dt.float32
+BF16 = mybir.dt.bfloat16
+I32 = mybir.dt.int32
+U32 = mybir.dt.uint32
+U16 = mybir.dt.uint16
+U8 = mybir.dt.uint8
+FP8X4 = mybir.dt.float8_e4m3fn_x4
+FP4X4 = mybir.dt.float4_e2m1fn_x4
+GELU = mybir.ActivationFunctionType.Gelu_apprx_tanh
+MULT = mybir.AluOpType.mult
+
+P = 128
+PASS = 512
+HALVES = H // PASS
+N_TILES = N // P
+
+
+GROUP = 2
+
+
+def load_scale_rows(queue, plane, rows):
+    for j in range(4):
+        queue.dma_start(out=plane[j:P:32].bitcast(I32), in_=rows[j].bitcast(I32))
+
+
+def tile_moe_pke_glu_gelu_kernel(
+    tc, x_words, x_scales, w1_words, w1_scales, w3_words, w3_scales, w2_words, w2_scales, offs, out
+):
+    nc = tc.nc
+    with ExitStack() as ctx:
+        keep = ctx.enter_context(tc.tile_pool(name="keep", bufs=1))
+        work = ctx.enter_context(tc.tile_pool(name="work", bufs=2))
+        psum = ctx.enter_context(tc.psum_pool(name="psum", bufs=2))
+
+        def slot(tag, name, width, dtype=U8):
+            return keep.tile([P, width], dtype, name=name, tag=tag, align_bytes=64)
+
+        def load_words(dst, src):
+            nc.sync.dma_start(out=dst.bitcast(I32), in_=src.bitcast(I32))
+
+        def load_second(dst, e):
+            load_words(dst.rearrange("p (s n) -> p s n", s=HALVES), w2_words[e].rearrange("s p n -> p s n"))
+
+        def first_rows(scales, g):
+            return scales[GROUP * g : GROUP * (g + 1)].rearrange("e s (q j) i -> j q (e s) i", j=4)
+
+        def load_first_plane(plane, scales, g):
+            load_scale_rows(nc.sync, plane.rearrange("p (e i) -> p e i", e=GROUP), first_rows(scales, g))
+
+        ROW = 2 * H
+        offsets = keep.tile([P, E * C // 16], U16, name="offsets")
+        x_tab = slot("x_tab", "x_tab", T, I32)
+        x_plane = slot("x_plane", "x_plane", T)
+        w1_plane = {0: slot("w1_plane", "w1_plane0", GROUP * H)[:]}
+        w3_plane = {0: slot("w3_plane", "w3_plane0", GROUP * H)[:]}
+        w2_plane = keep.tile([P, E * HALVES, N], U8, name="w2_plane", align_bytes=64)
+        w1 = {0: slot("w1", "w1_0", ROW)[:]}
+        w3 = {0: slot("w3", "w3_0", ROW)[:]}
+        w2 = {}
+        ident = keep.tile([P, P], F32, name="ident")
+        warm = keep.tile([P, 8], F32, name="warm")
+
+        nc.vector.memset(x_plane[:].bitcast(I32), 0)
+        nc.vector.memset(w1_plane[0].bitcast(I32), 0)
+        nc.vector.memset(w3_plane[0].bitcast(I32), 0)
+        nc.vector.memset(w2_plane[:].bitcast(I32), 0)
+        make_identity(nc, ident[:])
+        nc.scalar.activation(warm[:], ident[:, 0:8], GELU)
+
+        nc.sync.dma_start(offsets[:], offs)
+        load_scale_rows(nc.sync, x_plane, x_scales[0].rearrange("(q j) t -> j q t", j=4))
+        nc.sync.dma_start(out=x_tab[:], in_=x_words[0].rearrange("p t r -> p (t r)").bitcast(I32))
+        load_words(w1[0], w1_words[0, 0])
+        load_first_plane(w1_plane[0], w1_scales, 0)
+        load_words(w3[0], w3_words[0, 0])
+        load_first_plane(w3_plane[0], w3_scales, 0)
+        load_scale_rows(nc.gpsimd, w2_plane, w2_scales.rearrange("e s (q j) n -> j q (e s) n", j=4))
+
+        slot_plane = keep.tile([P, E * C], U8, name="slot_plane", align_bytes=64)
+        nc.vector.tensor_copy(slot_plane[:], x_plane[:].indirect(offsets[:]))
+
+        later = slot("x_plane", "later", 6 * ROW)
+        parts = [later[:, i * ROW : (i + 1) * ROW] for i in range(6)]
+        w1[1], w3[1], w2[0], w2[1], w1_plane[1], w3_plane[1] = parts
+        load_words(w1[1], w1_words[1, 0])
+        load_words(w3[1], w3_words[1, 0])
+        load_second(w2[0], 0)
+        load_second(w2[1], 1)
+
+        slot_words = []
+        for e in range(E):
+            words = keep.tile([P, C], U32, name="slot_words_%d" % e, align_bytes=64)
+            cols = slice(e * C // 16, (e + 1) * C // 16)
+            nc.vector.tensor_copy(words[:], x_tab[:].bitcast(U32).indirect(offsets[:, cols]))
+            slot_words.append(words)
+
+        third = slot("x_tab", "third", 2 * ROW)
+        w1[2], w3[2] = third[:, :ROW], third[:, ROW:]
+        load_words(w1[2], w1_words[2, 0])
+        load_words(w3[2], w3_words[2, 0])
+        nc.vector.memset(w1_plane[1].bitcast(I32), 0)
+        nc.vector.memset(w3_plane[1].bitcast(I32), 0)
+        load_first_plane(w1_plane[1], w1_scales, 1)
+        load_first_plane(w3_plane[1], w3_scales, 1)
+
+        staged = keep.tile([P, N_TILES, E * C], F32, name="staged")
+
+        def hidden(e, s):
+            sums = []
+            for tag, words, plane in (("a", w1, w1_plane), ("b", w3, w3_plane)):
+                acc = psum.tile([P, PASS], F32, name=tag)
+                i0 = (e % GROUP) * H + PASS * s
+                nc.tensor.matmul_mx(
+                    out=acc[:],
+                    lhsT=slot_words[e][:].bitcast(FP8X4),
+                    lhsT_scale=slot_plane[:, e * C : (e + 1) * C],
+                    rhs=words[e][:, 2 * PASS * s : 2 * PASS * (s + 1)].bitcast(FP4X4),
+                    rhs_scale=plane[e // GROUP][:, i0 : i0 + PASS],
+                    start=True,
+                    stop=True,
+                )
+                sums.append(acc[:].rearrange("c (p u d) -> c u p d", u=2, d=2))
+            act = work.tile([P, PASS], F32, name="act", bufs=4)
+            act_view = act[:].rearrange("c (u p d) -> c u p d", u=2, d=2)
+            nc.scalar.activation(act_view, sums[0], GELU)
+            h = work.tile([P, PASS], BF16, name="h", bufs=3, align_bytes=64)
+            nc.vector.tensor_tensor(h[:].rearrange("c (u p d) -> c u p d", u=2, d=2), sums[1], act_view, MULT)
+            return h
+
+        def quantise(h):
+            turned = psum.tile([P, 2, C], F32, name="turned")
+            pairs = h[:].bitcast(F32)
+            for u in range(2):
+                nc.tensor.transpose(turned[:, u, :], pairs[:, u * P : (u + 1) * P], ident[:])
+            grouped = work.tile([P, 4 * C], BF16, name="grouped", bufs=3, align_bytes=64)
+            nc.scalar.copy(
+                grouped[:].bitcast(F32).rearrange("p (c u) -> p c u", u=2),
+                turned[:].rearrange("p u c -> p c u"),
+            )
+            codes = work.tile([P, C], U32, name="codes", bufs=4, align_bytes=64)
+            scales = work.tile([P, C], U8, name="scales", bufs=4, align_bytes=64)
+            nc.vector.quantize_mx(out=codes[:].bitcast(FP8X4), scales=scales[:], in_=grouped[:])
+            return codes, scales
+
+        def second_pass(y, e, t, s, quantised):
+            codes, scales = quantised
+            nc.tensor.matmul_mx(
+                out=y,
+                lhsT=w2[e][:, 2 * (s * N + t * P) : 2 * (s * N + (t + 1) * P)].bitcast(FP4X4),
+                lhsT_scale=w2_plane[:, e * HALVES + s, t * P : (t + 1) * P],
+                rhs=codes[:].bitcast(FP8X4),
+                rhs_scale=scales[:],
+                start=(s == 0),
+                stop=(s == HALVES - 1),
+            )
+
+        def copy_out(e, t0, y, tiles, engine):
+            dst = staged[:, t0 : t0 + tiles, :].rearrange("p t (m e u) -> p t m e u", m=R, e=E)[:, :, :, e, :]
+            src = y[:].rearrange("p t (m u) -> p t m u", m=R)
+            if engine == 0:
+                nc.scalar.copy(dst, src)
+            else:
+                nc.vector.tensor_copy(dst, src)
+
+        def project(e, quantised):
+            for g in range(2):
+                y = psum.tile([P, 2, C], F32, name="y%d" % g, bufs=1)
+                for t in range(2):
+                    for s in range(HALVES):
+                        second_pass(y[:, t, :], e, 2 * g + t, s, quantised[s])
+                copy_out(e, 2 * g, y, 2, g)
+
+        def project_last(e, quantised):
+            banks = [
+                psum.tile([P, 1, C], F32, name="last%d" % t, tag=tag, bufs=bufs)
+                for t, (tag, bufs) in enumerate((("y0", 1), ("y1", 1), ("a", 2), ("b", 2)))
+            ]
+            for s in range(HALVES):
+                for t in range(N_TILES):
+                    second_pass(banks[t][:, 0, :], e, t, s, quantised[s])
+            for t in range(N_TILES):
+                copy_out(e, t, banks[t], 1, t % 2)
+                nc.sync.dma_start(out=out[t * P : (t + 1) * P, :], in_=staged[:, t, :])
+
+        units = [(e, s) for e in range(E) for s in range(HALVES)]
+        made = {}
+        quantised = {}
+        for step in range(len(units) + 2):
+            if step < len(units):
+                made[step] = hidden(*units[step])
+            if step == 1:
+                w1[3] = slot("w1", "w1_3", ROW)[:]
+                w3[3] = slot("w3", "w3_3", ROW)[:]
+                load_words(w1[3], w1_words[3, 0])
+                load_words(w3[3], w3_words[3, 0])
+            if step == 3:
+                w2[2] = slot("w1_plane", "w2_2", ROW)[:]
+                w2[3] = slot("w3_plane", "w2_3", ROW)[:]
+                load_second(w2[2], 2)
+                load_second(w2[3], 3)
+            if 1 <= step <= len(units):
+                quantised[step - 1] = quantise(made[step - 1])
+            if step >= 2 and units[step - 2][1] == HALVES - 1:
+                e = units[step - 2][0]
+                pair = [quantised[step - 3], quantised[step - 2]]
+                if e < E - 1:
+                    project(e, pair)
+                else:
+                    project_last(e, pair)

@@ -24,9 +24,6 @@ HALVES = H // PASS
 N_TILES = N // P
 
 
-GROUP = 2
-
-
 def load_scale_rows(queue, plane, rows):
     for j in range(4):
         queue.dma_start(out=plane[j:P:32].bitcast(I32), in_=rows[j].bitcast(I32))
@@ -50,51 +47,45 @@ def tile_moe_pke_glu_gelu_kernel(
         def load_second(dst, e):
             load_words(dst.rearrange("p (s n) -> p s n", s=HALVES), w2_words[e].rearrange("s p n -> p s n"))
 
-        def first_rows(scales, g):
-            return scales[GROUP * g : GROUP * (g + 1)].rearrange("e s (q j) i -> j q (e s) i", j=4)
-
-        def load_first_plane(plane, scales, g):
-            load_scale_rows(nc.sync, plane.rearrange("p (e i) -> p e i", e=GROUP), first_rows(scales, g))
-
         ROW = 2 * H
         offsets = keep.tile([P, E * C // 16], U16, name="offsets")
         x_tab = slot("x_tab", "x_tab", T, I32)
         x_plane = slot("x_plane", "x_plane", T)
-        w1_plane = {0: slot("w1_plane", "w1_plane0", GROUP * H)[:]}
-        w3_plane = {0: slot("w3_plane", "w3_plane0", GROUP * H)[:]}
-        w2_plane = keep.tile([P, E * HALVES, N], U8, name="w2_plane", align_bytes=64)
+        w1_plane = keep.tile([P, E, H], U8, name="w1_plane", align_bytes=64)
+        w3_plane = keep.tile([P, E, H], U8, name="w3_plane", align_bytes=64)
         w1 = {0: slot("w1", "w1_0", ROW)[:]}
         w3 = {0: slot("w3", "w3_0", ROW)[:]}
         w2 = {}
         ident = keep.tile([P, P], F32, name="ident")
         warm = keep.tile([P, 8], F32, name="warm")
 
-        nc.vector.memset(x_plane[:].bitcast(I32), 0)
-        nc.vector.memset(w1_plane[0].bitcast(I32), 0)
-        nc.vector.memset(w3_plane[0].bitcast(I32), 0)
-        nc.vector.memset(w2_plane[:].bitcast(I32), 0)
+        nc.vector.memset(w1_plane[:].bitcast(I32), 0)
+        nc.vector.memset(w3_plane[:].bitcast(I32), 0)
         make_identity(nc, ident[:])
         nc.scalar.activation(warm[:], ident[:, 0:8], GELU)
 
         nc.sync.dma_start(offsets[:], offs)
-        load_scale_rows(nc.sync, x_plane, x_scales[0].rearrange("(q j) t -> j q t", j=4))
+        for q in range(4):
+            rows = x_scales[0, 4 * q : 4 * q + 4, :].bitcast(I32)
+            nc.sync.dma_start(
+                out=x_plane[32 * q : 32 * q + 32, :].bitcast(I32),
+                in_=rows.unsqueeze(0).broadcast_to([8, 4, T // 4]),
+            )
         nc.sync.dma_start(out=x_tab[:], in_=x_words[0].rearrange("p t r -> p (t r)").bitcast(I32))
         load_words(w1[0], w1_words[0, 0])
-        load_first_plane(w1_plane[0], w1_scales, 0)
         load_words(w3[0], w3_words[0, 0])
-        load_first_plane(w3_plane[0], w3_scales, 0)
-        load_scale_rows(nc.gpsimd, w2_plane, w2_scales.rearrange("e s (q j) n -> j q (e s) n", j=4))
+        load_scale_rows(nc.sync, w1_plane, w1_scales.rearrange("e s (q j) i -> j q (e s) i", j=4))
+        load_scale_rows(nc.sync, w3_plane, w3_scales.rearrange("e s (q j) i -> j q (e s) i", j=4))
 
         slot_plane = keep.tile([P, E * C], U8, name="slot_plane", align_bytes=64)
         nc.vector.tensor_copy(slot_plane[:], x_plane[:].indirect(offsets[:]))
 
-        later = slot("x_plane", "later", 6 * ROW)
-        parts = [later[:, i * ROW : (i + 1) * ROW] for i in range(6)]
-        w1[1], w3[1], w2[0], w2[1], w1_plane[1], w3_plane[1] = parts
+        second = slot("x_plane", "second", 5 * ROW)
+        w1[1], w3[1], w2[0] = [second[:, i * ROW : (i + 1) * ROW] for i in range(3)]
+        w2_plane = second[:, 3 * ROW :].rearrange("p (g n) -> p g n", n=N)
         load_words(w1[1], w1_words[1, 0])
         load_words(w3[1], w3_words[1, 0])
         load_second(w2[0], 0)
-        load_second(w2[1], 1)
 
         slot_words = []
         for e in range(E):
@@ -102,54 +93,66 @@ def tile_moe_pke_glu_gelu_kernel(
             cols = slice(e * C // 16, (e + 1) * C // 16)
             nc.vector.tensor_copy(words[:], x_tab[:].bitcast(U32).indirect(offsets[:, cols]))
             slot_words.append(words)
+            if e == 0:
+                nc.vector.memset(w2_plane.bitcast(I32), 0)
+                load_scale_rows(nc.sync, w2_plane, w2_scales.rearrange("e s (q j) n -> j q (e s) n", j=4))
 
-        third = slot("x_tab", "third", 2 * ROW)
-        w1[2], w3[2] = third[:, :ROW], third[:, ROW:]
-        load_words(w1[2], w1_words[2, 0])
-        load_words(w3[2], w3_words[2, 0])
-        nc.vector.memset(w1_plane[1].bitcast(I32), 0)
-        nc.vector.memset(w3_plane[1].bitcast(I32), 0)
-        load_first_plane(w1_plane[1], w1_scales, 1)
-        load_first_plane(w3_plane[1], w3_scales, 1)
+        third = slot("x_tab", "third", 7 * ROW)
+        w1[2], w3[2], w2[1], w1[3], w3[3], w2[2], w2[3] = [third[:, i * ROW : (i + 1) * ROW] for i in range(7)]
+        for e in range(2, E):
+            load_words(w1[e], w1_words[e, 0])
+            load_words(w3[e], w3_words[e, 0])
+            load_second(w2[e - 1], e - 1)
+        load_second(w2[E - 1], E - 1)
 
         staged = keep.tile([P, N_TILES, E * C], F32, name="staged")
 
-        def hidden(e, s):
+        def first_sums(e, s):
             sums = []
             for tag, words, plane in (("a", w1, w1_plane), ("b", w3, w3_plane)):
                 acc = psum.tile([P, PASS], F32, name=tag)
-                i0 = (e % GROUP) * H + PASS * s
                 nc.tensor.matmul_mx(
                     out=acc[:],
                     lhsT=slot_words[e][:].bitcast(FP8X4),
                     lhsT_scale=slot_plane[:, e * C : (e + 1) * C],
                     rhs=words[e][:, 2 * PASS * s : 2 * PASS * (s + 1)].bitcast(FP4X4),
-                    rhs_scale=plane[e // GROUP][:, i0 : i0 + PASS],
+                    rhs_scale=plane[:, e, PASS * s : PASS * (s + 1)],
                     start=True,
                     stop=True,
                 )
                 sums.append(acc[:].rearrange("c (p u d) -> c u p d", u=2, d=2))
+            return sums
+
+        def gate(sums, h, pieces):
             act = work.tile([P, PASS], F32, name="act", bufs=4)
             act_view = act[:].rearrange("c (u p d) -> c u p d", u=2, d=2)
-            nc.scalar.activation(act_view, sums[0], GELU)
-            h = work.tile([P, PASS], BF16, name="h", bufs=3, align_bytes=64)
-            nc.vector.tensor_tensor(h[:].rearrange("c (u p d) -> c u p d", u=2, d=2), sums[1], act_view, MULT)
+            h_view = h.rearrange("c (u p d) -> c u p d", u=2, d=2)
+            for us in pieces:
+                nc.scalar.activation(act_view[:, us], sums[0][:, us], GELU)
+                nc.vector.tensor_tensor(h_view[:, us], sums[1][:, us], act_view[:, us], MULT)
+
+        def hidden(e, halves, pieces):
+            h = work.tile([P, len(halves), PASS], BF16, name="h", bufs=3, align_bytes=64)
+            for i, s in enumerate(halves):
+                gate(first_sums(e, s), h[:, i, :], pieces)
             return h
 
         def quantise(h):
-            turned = psum.tile([P, 2, C], F32, name="turned")
-            pairs = h[:].bitcast(F32)
-            for u in range(2):
-                nc.tensor.transpose(turned[:, u, :], pairs[:, u * P : (u + 1) * P], ident[:])
-            grouped = work.tile([P, 4 * C], BF16, name="grouped", bufs=3, align_bytes=64)
+            n = h.shape[1]
+            turned = psum.tile([P, n, 2, C], F32, name="turned")
+            for i in range(n):
+                pairs = h[:, i, :].bitcast(F32)
+                for u in range(2):
+                    nc.tensor.transpose(turned[:, i, u, :], pairs[:, u * P : (u + 1) * P], ident[:])
+            grouped = work.tile([P, n * 4 * C], BF16, name="grouped", bufs=3, align_bytes=64)
             nc.scalar.copy(
-                grouped[:].bitcast(F32).rearrange("p (c u) -> p c u", u=2),
-                turned[:].rearrange("p u c -> p c u"),
+                grouped[:].bitcast(F32).rearrange("p (i c u) -> p i c u", i=n, u=2),
+                turned[:].rearrange("p i u c -> p i c u"),
             )
-            codes = work.tile([P, C], U32, name="codes", bufs=4, align_bytes=64)
-            scales = work.tile([P, C], U8, name="scales", bufs=4, align_bytes=64)
+            codes = work.tile([P, n * C], U32, name="codes", bufs=3, align_bytes=64)
+            scales = work.tile([P, n * C], U8, name="scales", bufs=3, align_bytes=64)
             nc.vector.quantize_mx(out=codes[:].bitcast(FP8X4), scales=scales[:], in_=grouped[:])
-            return codes, scales
+            return [(codes[:, i * C : (i + 1) * C], scales[:, i * C : (i + 1) * C]) for i in range(n)]
 
         def second_pass(y, e, t, s, quantised):
             codes, scales = quantised
@@ -157,8 +160,8 @@ def tile_moe_pke_glu_gelu_kernel(
                 out=y,
                 lhsT=w2[e][:, 2 * (s * N + t * P) : 2 * (s * N + (t + 1) * P)].bitcast(FP4X4),
                 lhsT_scale=w2_plane[:, e * HALVES + s, t * P : (t + 1) * P],
-                rhs=codes[:].bitcast(FP8X4),
-                rhs_scale=scales[:],
+                rhs=codes.bitcast(FP8X4),
+                rhs_scale=scales,
                 start=(s == 0),
                 stop=(s == HALVES - 1),
             )
@@ -172,18 +175,14 @@ def tile_moe_pke_glu_gelu_kernel(
                 nc.vector.tensor_copy(dst, src)
 
         def project(e, quantised):
-            for g in range(2):
-                y = psum.tile([P, 2, C], F32, name="y%d" % g, bufs=1)
-                for t in range(2):
-                    for s in range(HALVES):
-                        second_pass(y[:, t, :], e, 2 * g + t, s, quantised[s])
-                copy_out(e, 2 * g, y, 2, g)
+            y = psum.tile([P, N_TILES, C], F32, name="y")
+            for t in range(N_TILES):
+                for s in range(HALVES):
+                    second_pass(y[:, t, :], e, t, s, quantised[s])
+            copy_out(e, 0, y, N_TILES, min(e, 1))
 
         def project_last(e, quantised):
-            banks = [
-                psum.tile([P, 1, C], F32, name="last%d" % t, tag=tag, bufs=bufs)
-                for t, (tag, bufs) in enumerate((("y0", 1), ("y1", 1), ("a", 2), ("b", 2)))
-            ]
+            banks = [psum.tile([P, 1, C], F32, name="last%d" % t, tag=tag) for t, tag in enumerate(("a", "b", "y", "a"))]
             for s in range(HALVES):
                 for t in range(N_TILES):
                     second_pass(banks[t][:, 0, :], e, t, s, quantised[s])
@@ -191,28 +190,17 @@ def tile_moe_pke_glu_gelu_kernel(
                 copy_out(e, t, banks[t], 1, t % 2)
                 nc.sync.dma_start(out=out[t * P : (t + 1) * P, :], in_=staged[:, t, :])
 
-        units = [(e, s) for e in range(E) for s in range(HALVES)]
-        made = {}
-        quantised = {}
-        for step in range(len(units) + 2):
-            if step < len(units):
-                made[step] = hidden(*units[step])
-            if step == 1:
-                w1[3] = slot("w1", "w1_3", ROW)[:]
-                w3[3] = slot("w3", "w3_3", ROW)[:]
-                load_words(w1[3], w1_words[3, 0])
-                load_words(w3[3], w3_words[3, 0])
-            if step == 3:
-                w2[2] = slot("w1_plane", "w2_2", ROW)[:]
-                w2[3] = slot("w3_plane", "w2_3", ROW)[:]
-                load_second(w2[2], 2)
-                load_second(w2[3], 3)
-            if 1 <= step <= len(units):
-                quantised[step - 1] = quantise(made[step - 1])
-            if step >= 2 and units[step - 2][1] == HALVES - 1:
-                e = units[step - 2][0]
-                pair = [quantised[step - 3], quantised[step - 2]]
-                if e < E - 1:
-                    project(e, pair)
-                else:
-                    project_last(e, pair)
+        whole = [slice(0, 2)]
+        split = [slice(0, 1), slice(1, 2)]
+        h = hidden(0, range(HALVES), whole)
+        for e in range(1, E - 1):
+            h_next = hidden(e, range(HALVES), whole)
+            project(e - 1, quantise(h))
+            h = h_next
+        h_low = hidden(E - 1, [0], whole)
+        h_high = hidden(E - 1, [1], split)
+        before_last = quantise(h)
+        low = quantise(h_low)
+        project(E - 2, before_last)
+        high = quantise(h_high)
+        project_last(E - 1, low + high)

@@ -36,7 +36,7 @@ def tile_moe_pke_glu_gelu_kernel(
     with ExitStack() as ctx:
         keep = ctx.enter_context(tc.tile_pool(name="keep", bufs=1))
         work = ctx.enter_context(tc.tile_pool(name="work", bufs=2))
-        psum = ctx.enter_context(tc.psum_pool(name="psum", bufs=2))
+        psum = ctx.enter_context(tc.psum_pool(name="psum", bufs=1))
 
         def slot(tag, name, width, dtype=U8):
             return keep.tile([P, width], dtype, name=name, tag=tag, align_bytes=64)
@@ -49,8 +49,6 @@ def tile_moe_pke_glu_gelu_kernel(
 
         ROW = 2 * H
         offsets = keep.tile([P, E * C // 16], U16, name="offsets")
-        x_tab = slot("x_tab", "x_tab", T, I32)
-        x_plane = slot("x_plane", "x_plane", T)
         w1_plane = keep.tile([P, E, H], U8, name="w1_plane", align_bytes=64)
         w3_plane = keep.tile([P, E, H], U8, name="w3_plane", align_bytes=64)
         w1 = {0: slot("w1", "w1_0", ROW)[:]}
@@ -64,53 +62,47 @@ def tile_moe_pke_glu_gelu_kernel(
         make_identity(nc, ident[:])
         nc.scalar.activation(warm[:], ident[:, 0:8], GELU)
 
-        nc.sync.dma_start(offsets[:], offs)
-        for q in range(4):
-            rows = x_scales[0, 4 * q : 4 * q + 4, :].bitcast(I32)
-            nc.sync.dma_start(
-                out=x_plane[32 * q : 32 * q + 32, :].bitcast(I32),
-                in_=rows.unsqueeze(0).broadcast_to([8, 4, T // 4]),
-            )
-        nc.sync.dma_start(out=x_tab[:], in_=x_words[0].rearrange("p t r -> p (t r)").bitcast(I32))
-        load_words(w1[0], w1_words[0, 0])
-        load_words(w3[0], w3_words[0, 0])
-        load_scale_rows(nc.sync, w1_plane, w1_scales.rearrange("e s (q j) i -> j q (e s) i", j=4))
-        load_scale_rows(nc.sync, w3_plane, w3_scales.rearrange("e s (q j) i -> j q (e s) i", j=4))
-
         slot_plane = keep.tile([P, E * C], U8, name="slot_plane", align_bytes=64)
-        nc.vector.tensor_copy(slot_plane[:], x_plane[:].indirect(offsets[:]))
+        slot_words = [keep.tile([P, C], U32, name="slot_words_%d" % e, align_bytes=64) for e in range(E)]
+        staged = keep.tile([P, N_TILES, E * C], F32, name="staged")
+        with tc.tile_pool(name="tokens", bufs=1) as tokens:
+            x_tab = tokens.tile([P, T], I32, name="x_tab", align_bytes=64)
+            x_plane = tokens.tile([P, T], U8, name="x_plane", align_bytes=64)
+            nc.sync.dma_start(offsets[:], offs)
+            for q in range(4):
+                rows = x_scales[0, 4 * q : 4 * q + 4, :].bitcast(I32)
+                nc.sync.dma_start(
+                    out=x_plane[32 * q : 32 * q + 32, :].bitcast(I32),
+                    in_=rows.unsqueeze(0).broadcast_to([8, 4, T // 4]),
+                )
+            nc.sync.dma_start(out=x_tab[:], in_=x_words[0].rearrange("p t r -> p (t r)").bitcast(I32))
+            load_words(w1[0], w1_words[0, 0])
+            load_words(w3[0], w3_words[0, 0])
+            load_scale_rows(nc.sync, w1_plane, w1_scales.rearrange("e s (q j) i -> j q (e s) i", j=4))
+            load_scale_rows(nc.sync, w3_plane, w3_scales.rearrange("e s (q j) i -> j q (e s) i", j=4))
 
-        second = slot("x_plane", "second", 5 * ROW)
-        w1[1], w3[1], w2[0] = [second[:, i * ROW : (i + 1) * ROW] for i in range(3)]
-        w2_plane = second[:, 3 * ROW :].rearrange("p (g n) -> p g n", n=N)
-        load_words(w1[1], w1_words[1, 0])
-        load_words(w3[1], w3_words[1, 0])
-        load_second(w2[0], 0)
+            nc.vector.tensor_copy(slot_plane[:], x_plane[:].indirect(offsets[:]))
+            for e in range(E):
+                cols = slice(e * C // 16, (e + 1) * C // 16)
+                nc.vector.tensor_copy(slot_words[e][:], x_tab[:].bitcast(U32).indirect(offsets[:, cols]))
 
-        slot_words = []
-        for e in range(E):
-            words = keep.tile([P, C], U32, name="slot_words_%d" % e, align_bytes=64)
-            cols = slice(e * C // 16, (e + 1) * C // 16)
-            nc.vector.tensor_copy(words[:], x_tab[:].bitcast(U32).indirect(offsets[:, cols]))
-            slot_words.append(words)
-            if e == 0:
-                nc.vector.memset(w2_plane.bitcast(I32), 0)
-                load_scale_rows(nc.sync, w2_plane, w2_scales.rearrange("e s (q j) n -> j q (e s) n", j=4))
-
-        third = slot("x_tab", "third", 7 * ROW)
-        w1[2], w3[2], w2[1], w1[3], w3[3], w2[2], w2[3] = [third[:, i * ROW : (i + 1) * ROW] for i in range(7)]
-        for e in range(2, E):
+        later = ctx.enter_context(tc.tile_pool(name="later", bufs=1))
+        for e in range(1, E):
+            w1[e] = later.tile([P, ROW], U8, name="w1_%d" % e, align_bytes=64)[:]
+            w3[e] = later.tile([P, ROW], U8, name="w3_%d" % e, align_bytes=64)[:]
             load_words(w1[e], w1_words[e, 0])
             load_words(w3[e], w3_words[e, 0])
-            load_second(w2[e - 1], e - 1)
-        load_second(w2[E - 1], E - 1)
+        w2[0] = later.tile([P, ROW], U8, name="w2_0", align_bytes=64)[:]
+        w2_plane = later.tile([P, E * HALVES, N], U8, name="w2_plane", align_bytes=64)
+        load_second(w2[0], 0)
+        nc.vector.memset(w2_plane[:].bitcast(I32), 0)
+        load_scale_rows(nc.sync, w2_plane, w2_scales.rearrange("e s (q j) n -> j q (e s) n", j=4))
 
-        staged = keep.tile([P, N_TILES, E * C], F32, name="staged")
 
         def first_sums(e, s):
             sums = []
             for tag, words, plane in (("a", w1, w1_plane), ("b", w3, w3_plane)):
-                acc = psum.tile([P, PASS], F32, name=tag)
+                acc = psum.tile([P, PASS], F32, name="sum_" + tag, tag="%s%d" % (tag, (HALVES * e + s) % 4))
                 nc.tensor.matmul_mx(
                     out=acc[:],
                     lhsT=slot_words[e][:].bitcast(FP8X4),
@@ -132,25 +124,25 @@ def tile_moe_pke_glu_gelu_kernel(
                 nc.vector.tensor_tensor(h_view[:, us], sums[1][:, us], act_view[:, us], MULT)
 
         def hidden(e, halves, pieces):
-            h = work.tile([P, len(halves), PASS], BF16, name="h", bufs=3, align_bytes=64)
+            h = work.tile([P, len(halves), PASS], BF16, name="h", bufs=E, align_bytes=64)
             for i, s in enumerate(halves):
                 gate(first_sums(e, s), h[:, i, :], pieces)
             return h
 
-        def quantise(h):
+        def quantise(e, h):
             n = h.shape[1]
-            turned = psum.tile([P, n, 2, C], F32, name="turned")
+            turned = psum.tile([P, n, 2, C], F32, name="turned", tag="a%d" % e)
             for i in range(n):
                 pairs = h[:, i, :].bitcast(F32)
                 for u in range(2):
                     nc.tensor.transpose(turned[:, i, u, :], pairs[:, u * P : (u + 1) * P], ident[:])
-            grouped = work.tile([P, n * 4 * C], BF16, name="grouped", bufs=3, align_bytes=64)
+            grouped = work.tile([P, n * 4 * C], BF16, name="grouped", bufs=E, align_bytes=64)
             nc.scalar.copy(
                 grouped[:].bitcast(F32).rearrange("p (i c u) -> p i c u", i=n, u=2),
                 turned[:].rearrange("p i u c -> p i c u"),
             )
-            codes = work.tile([P, n * C], U32, name="codes", bufs=3, align_bytes=64)
-            scales = work.tile([P, n * C], U8, name="scales", bufs=3, align_bytes=64)
+            codes = work.tile([P, n * C], U32, name="codes", bufs=E, align_bytes=64)
+            scales = work.tile([P, n * C], U8, name="scales", bufs=E, align_bytes=64)
             nc.vector.quantize_mx(out=codes[:].bitcast(FP8X4), scales=scales[:], in_=grouped[:])
             return [(codes[:, i * C : (i + 1) * C], scales[:, i * C : (i + 1) * C]) for i in range(n)]
 
@@ -175,32 +167,31 @@ def tile_moe_pke_glu_gelu_kernel(
                 nc.vector.tensor_copy(dst, src)
 
         def project(e, quantised):
-            y = psum.tile([P, N_TILES, C], F32, name="y")
+            y = psum.tile([P, N_TILES, C], F32, name="y", tag="b%d" % (e + 1))
             for t in range(N_TILES):
                 for s in range(HALVES):
                     second_pass(y[:, t, :], e, t, s, quantised[s])
-            copy_out(e, 0, y, N_TILES, min(e, 1))
+            copy_out(e, 0, y, N_TILES, e % 2)
 
         def project_last(e, quantised):
-            banks = [psum.tile([P, 1, C], F32, name="last%d" % t, tag=tag) for t, tag in enumerate(("a", "b", "y", "a"))]
-            for s in range(HALVES):
-                for t in range(N_TILES):
-                    second_pass(banks[t][:, 0, :], e, t, s, quantised[s])
+            banks = [psum.tile([P, 1, C], F32, name="last%d" % t, tag=tag) for t, tag in enumerate(("b0", "a0", "a1", "a2"))]
             for t in range(N_TILES):
+                for s in range(HALVES):
+                    second_pass(banks[t][:, 0, :], e, t, s, quantised[s])
                 copy_out(e, t, banks[t], 1, t % 2)
                 nc.sync.dma_start(out=out[t * P : (t + 1) * P, :], in_=staged[:, t, :])
 
         whole = [slice(0, 2)]
-        split = [slice(0, 1), slice(1, 2)]
-        h = hidden(0, range(HALVES), whole)
-        for e in range(1, E - 1):
-            h_next = hidden(e, range(HALVES), whole)
-            project(e - 1, quantise(h))
-            h = h_next
-        h_low = hidden(E - 1, [0], whole)
-        h_high = hidden(E - 1, [1], split)
-        before_last = quantise(h)
-        low = quantise(h_low)
-        project(E - 2, before_last)
-        high = quantise(h_high)
-        project_last(E - 1, low + high)
+        h = [hidden(e, range(HALVES), whole) for e in range(2)]
+        w2[1] = slot("w3", "w2_1", ROW)[:]
+        w2[2] = later.tile([P, ROW], U8, name="w2_2", tag="w1_1", align_bytes=64)[:]
+        w2[3] = later.tile([P, ROW], U8, name="w2_3", tag="w3_1", align_bytes=64)[:]
+        for e in range(1, E):
+            load_second(w2[e], e)
+        h.extend(hidden(e, range(HALVES), whole) for e in range(2, E))
+        made = quantise(0, h[0])
+        for e in range(1, E):
+            ahead = quantise(e, h[e])
+            project(e - 1, made)
+            made = ahead
+        project_last(E - 1, made)

from contextlib import ExitStack

import concourse.mybir as mybir
from concourse.masks import make_identity

K, T, E, C, H, N = 512, 1024, 4, 128, 1024, 512
R = 4
FLOPS = 2 * E * C * (2 * K * H + H * N)

F32 = mybir.dt.float32
BF16 = mybir.dt.bfloat16
I32 = mybir.dt.int32
U32 = mybir.dt.uint32
U16 = mybir.dt.uint16
U8 = mybir.dt.uint8
FP8X4 = mybir.dt.float8_e4m3fn_x4
FP4X4 = mybir.dt.float4_e2m1fn_x4
GELU = mybir.ActivationFunctionType.Gelu_apprx_tanh
MULT = mybir.AluOpType.mult

P = 128
PASS = 512
HALVES = H // PASS
N_TILES = N // P


def load_scale_rows(queue, plane, rows):
    for j in range(4):
        queue.dma_start(out=plane[j:P:32].bitcast(I32), in_=rows[j].bitcast(I32))


def tile_moe_pke_glu_gelu_kernel(
    tc, x_words, x_scales, w1_words, w1_scales, w3_words, w3_scales, w2_words, w2_scales, offs, out
):
    nc = tc.nc
    with ExitStack() as ctx:
        keep = ctx.enter_context(tc.tile_pool(name="keep", bufs=1))
        work = ctx.enter_context(tc.tile_pool(name="work", bufs=2))
        psum = ctx.enter_context(tc.psum_pool(name="psum", bufs=1))

        def slot(tag, name, width, dtype=U8):
            return keep.tile([P, width], dtype, name=name, tag=tag, align_bytes=64)

        def load_words(dst, src):
            nc.sync.dma_start(out=dst.bitcast(I32), in_=src.bitcast(I32))

        def load_second(dst, e):
            load_words(dst.rearrange("p (s n) -> p s n", s=HALVES), w2_words[e].rearrange("s p n -> p s n"))

        ROW = 2 * H
        offsets = keep.tile([P, E * C // 16], U16, name="offsets")
        w1_plane = keep.tile([P, E, H], U8, name="w1_plane", align_bytes=64)
        w3_plane = keep.tile([P, E, H], U8, name="w3_plane", align_bytes=64)
        w1 = {0: slot("w1", "w1_0", ROW)[:]}
        w3 = {0: slot("w3", "w3_0", ROW)[:]}
        w2 = {}
        ident = keep.tile([P, P], F32, name="ident")
        warm = keep.tile([P, 8], F32, name="warm")

        nc.vector.memset(w1_plane[:].bitcast(I32), 0)
        nc.vector.memset(w3_plane[:].bitcast(I32), 0)
        make_identity(nc, ident[:])
        nc.scalar.activation(warm[:], ident[:, 0:8], GELU)

        slot_plane = keep.tile([P, E * C], U8, name="slot_plane", align_bytes=64)
        slot_words = [keep.tile([P, C], U32, name="slot_words_%d" % e, align_bytes=64) for e in range(E)]
        staged = keep.tile([P, N_TILES, E * C], F32, name="staged")
        with tc.tile_pool(name="tokens", bufs=1) as tokens:
            x_tab = tokens.tile([P, T], I32, name="x_tab", align_bytes=64)
            x_plane = tokens.tile([P, T], U8, name="x_plane", align_bytes=64)
            nc.sync.dma_start(offsets[:], offs)
            for q in range(4):
                rows = x_scales[0, 4 * q : 4 * q + 4, :].bitcast(I32)
                nc.sync.dma_start(
                    out=x_plane[32 * q : 32 * q + 32, :].bitcast(I32),
                    in_=rows.unsqueeze(0).broadcast_to([8, 4, T // 4]),
                )
            nc.sync.dma_start(out=x_tab[:], in_=x_words[0].rearrange("p t r -> p (t r)").bitcast(I32))
            load_words(w1[0], w1_words[0, 0])
            load_words(w3[0], w3_words[0, 0])
            load_scale_rows(nc.sync, w1_plane, w1_scales.rearrange("e s (q j) i -> j q (e s) i", j=4))
            load_scale_rows(nc.sync, w3_plane, w3_scales.rearrange("e s (q j) i -> j q (e s) i", j=4))

            nc.vector.tensor_copy(slot_plane[:], x_plane[:].indirect(offsets[:]))
            for e in range(E):
                cols = slice(e * C // 16, (e + 1) * C // 16)
                nc.vector.tensor_copy(slot_words[e][:], x_tab[:].bitcast(U32).indirect(offsets[:, cols]))

        later = ctx.enter_context(tc.tile_pool(name="later", bufs=1))
        for e in range(1, E):
            w1[e] = later.tile([P, ROW], U8, name="w1_%d" % e, align_bytes=64)[:]
            w3[e] = later.tile([P, ROW], U8, name="w3_%d" % e, align_bytes=64)[:]
            load_words(w1[e], w1_words[e, 0])
            load_words(w3[e], w3_words[e, 0])
        w2[0] = later.tile([P, ROW], U8, name="w2_0", align_bytes=64)[:]
        w2_plane = later.tile([P, E * HALVES, N], U8, name="w2_plane", align_bytes=64)
        load_second(w2[0], 0)
        nc.vector.memset(w2_plane[:].bitcast(I32), 0)
        load_scale_rows(nc.sync, w2_plane, w2_scales.rearrange("e s (q j) n -> j q (e s) n", j=4))


        def first_sums(e, s):
            sums = []
            for tag, words, plane in (("a", w1, w1_plane), ("b", w3, w3_plane)):
                acc = psum.tile([P, PASS], F32, name="sum_" + tag, tag="%s%d" % (tag, (HALVES * e + s) % 4))
                nc.tensor.matmul_mx(
                    out=acc[:],
                    lhsT=slot_words[e][:].bitcast(FP8X4),
                    lhsT_scale=slot_plane[:, e * C : (e + 1) * C],
                    rhs=words[e][:, 2 * PASS * s : 2 * PASS * (s + 1)].bitcast(FP4X4),
                    rhs_scale=plane[:, e, PASS * s : PASS * (s + 1)],
                    start=True,
                    stop=True,
                )
                sums.append(acc[:].rearrange("c (p u d) -> c u p d", u=2, d=2))
            return sums

        def gate(sums, h, pieces):
            act = work.tile([P, PASS], F32, name="act", bufs=4)
            act_view = act[:].rearrange("c (u p d) -> c u p d", u=2, d=2)
            h_view = h.rearrange("c (u p d) -> c u p d", u=2, d=2)
            for us in pieces:
                nc.scalar.activation(act_view[:, us], sums[0][:, us], GELU)
                nc.vector.tensor_tensor(h_view[:, us], sums[1][:, us], act_view[:, us], MULT)

        def hidden(e, halves, pieces):
            h = work.tile([P, len(halves), PASS], BF16, name="h", bufs=E, align_bytes=64)
            for i, s in enumerate(halves):
                gate(first_sums(e, s), h[:, i, :], pieces)
            return h

        def quantise(e, h):
            n = h.shape[1]
            turned = psum.tile([P, n, 2, C], F32, name="turned", tag="a%d" % e)
            for i in range(n):
                pairs = h[:, i, :].bitcast(F32)
                for u in range(2):
                    nc.tensor.transpose(turned[:, i, u, :], pairs[:, u * P : (u + 1) * P], ident[:])
            grouped = work.tile([P, n * 4 * C], BF16, name="grouped", bufs=E, align_bytes=64)
            nc.scalar.copy(
                grouped[:].bitcast(F32).rearrange("p (i c u) -> p i c u", i=n, u=2),
                turned[:].rearrange("p i u c -> p i c u"),
            )
            codes = work.tile([P, n * C], U32, name="codes", bufs=E, align_bytes=64)
            scales = work.tile([P, n * C], U8, name="scales", bufs=E, align_bytes=64)
            nc.vector.quantize_mx(out=codes[:].bitcast(FP8X4), scales=scales[:], in_=grouped[:])
            return [(codes[:, i * C : (i + 1) * C], scales[:, i * C : (i + 1) * C]) for i in range(n)]

        def second_pass(y, e, t, s, quantised):
            codes, scales = quantised
            nc.tensor.matmul_mx(
                out=y,
                lhsT=w2[e][:, 2 * (s * N + t * P) : 2 * (s * N + (t + 1) * P)].bitcast(FP4X4),
                lhsT_scale=w2_plane[:, e * HALVES + s, t * P : (t + 1) * P],
                rhs=codes.bitcast(FP8X4),
                rhs_scale=scales,
                start=(s == 0),
                stop=(s == HALVES - 1),
            )

        def copy_out(e, t0, y, tiles, engine):
            dst = staged[:, t0 : t0 + tiles, :].rearrange("p t (m e u) -> p t m e u", m=R, e=E)[:, :, :, e, :]
            src = y[:].rearrange("p t (m u) -> p t m u", m=R)
            if engine == 0:
                nc.scalar.copy(dst, src)
            else:
                nc.vector.tensor_copy(dst, src)

        def project(e, quantised):
            y = psum.tile([P, N_TILES, C], F32, name="y", tag="b%d" % (e + 1))
            for t in range(N_TILES):
                for s in range(HALVES):
                    second_pass(y[:, t, :], e, t, s, quantised[s])
            copy_out(e, 0, y, N_TILES, e % 2)

        def project_last(e, quantised):
            banks = [psum.tile([P, 1, C], F32, name="last%d" % t, tag=tag) for t, tag in enumerate(("b0", "a0", "a1", "a2"))]
            for t in range(N_TILES):
                for s in range(HALVES):
                    second_pass(banks[t][:, 0, :], e, t, s, quantised[s])
                copy_out(e, t, banks[t], 1, t % 2)
                nc.sync.dma_start(out=out[t * P : (t + 1) * P, :], in_=staged[:, t, :])

        whole = [slice(0, 2)]
        h = [hidden(e, range(HALVES), whole) for e in range(2)]
        w2[1] = slot("w3", "w2_1", ROW)[:]
        w2[2] = later.tile([P, ROW], U8, name="w2_2", tag="w1_1", align_bytes=64)[:]
        w2[3] = later.tile([P, ROW], U8, name="w2_3", tag="w3_1", align_bytes=64)[:]
        for e in range(1, E):
            load_second(w2[e], e)
        h.extend(hidden(e, range(HALVES), whole) for e in range(2, E))
        made = quantise(0, h[0])
        for e in range(1, E):
            ahead = quantise(e, h[e])
            project(e - 1, made)
            made = ahead
        project_last(E - 1, made)
